import numpy as np
import ml_dtypes


def mxq(x, axis, fmt="e4m3"):
    dtype, down = {"e4m3": (ml_dtypes.float8_e4m3fn, 7), "e5m2": (ml_dtypes.float8_e5m2, 14)}[fmt]
    v = np.moveaxis(np.asarray(x, np.float32).astype(ml_dtypes.bfloat16).astype(np.float64), axis, -1)
    blocks = v.reshape(v.shape[:-1] + (-1, 32))
    amax = np.abs(blocks).max(-1, keepdims=True)
    byte = np.maximum(np.where(amax > 0, np.frexp(amax)[1] - 1 + 127, 0) - down, 1)
    scale = np.exp2(byte - 127.0)
    codes = (blocks / scale).astype(np.float32).astype(dtype).astype(np.float64)
    return np.moveaxis((codes * scale).reshape(v.shape), -1, axis)


WIDE = False


def mx_kscale(k):
    if not WIDE:
        return np.ones(k)
    levels = np.array([30, -30])
    if k % 512:
        return np.exp2(np.random.permutation(np.resize(levels, k // 32))).repeat(32)
    a = np.empty((k // 512, 16))
    for p in range(k // 512):
        a[p, :8] = np.random.permutation(np.resize(levels, 8))
        for g in range(8):
            far = levels[np.abs(levels - a[p, g]) >= 10]
            a[p, g + 8] = far[np.random.randint(len(far))]
    return np.exp2(a.ravel()).repeat(32)


def f64(x):
    return np.asarray(x).astype(np.float64)


def striped(idx):
    return np.tile(np.asarray(idx).reshape(-1, 16).T, (8, 1)).astype(np.uint16)


def unstriped(offs):
    return offs[:16].T.reshape(-1).astype(np.int64)


K, N, T, J = 512, 512, 1024, 512


def setup_inputs():
    n = np.random.standard_normal
    idx = np.random.permutation(T)[:J]
    fj = mx_kscale(J)
    tj = np.ones(T)
    tj[idx] = fj
    return {
        "xt": (n((K, T)) * tj).astype(np.float32),
        "g": (n((N, T)) * np.exp(0.5 * n((1, T)))).astype(np.float32),
        "sv": (n((N, T))).astype(np.float32),
        "rb": (np.random.uniform(0.4, 1.2, (1, J)) / fj).astype(np.float32),
        "mom": (1.0 * n((K, N))).astype(np.float32),
        "offs": striped(idx),
    }


def reference(xt, g, sv, rb, mom, offs):
    idx = unstriped(offs)
    xj = f64(xt)[:, idx].T
    gs = f64(g)[:, idx] * f64(sv)[:, idx] * f64(rb)
    gj = gs.T
    xjq = mxq(xj, 0, "e4m3")
    gjq = mxq(gj, 0, "e5m2")
    w = xjq.T @ gjq
    y = 0.04 * w + 0.5 * f64(mom)
    return y

@@ -1,0 +1,137 @@
+from contextlib import ExitStack
+
+import concourse.mybir as mybir
+from concourse.masks import make_identity
+
+K, N, T, J = 512, 512, 1024, 512
+FLOPS = 2 * K * N * J
+
+F32 = mybir.dt.float32
+BF16 = mybir.dt.bfloat16
+U32 = mybir.dt.uint32
+U16 = mybir.dt.uint16
+U8 = mybir.dt.uint8
+E4M3 = mybir.dt.float8_e4m3fn_x4
+E5M2 = mybir.dt.float8_e5m2_x4
+MULT = mybir.AluOpType.mult
+ADD = mybir.AluOpType.add
+COPY = mybir.ActivationFunctionType.Copy
+
+P = 128
+BLOCKS = 4
+SCALAR_BLOCKS = 3
+
+
+def tile_moe_expert_wgrad_through_saved_kernel(tc, xt, g, sv, rb, mom, offs, out):
+    nc = tc.nc
+    with ExitStack() as ctx:
+        keep = ctx.enter_context(tc.tile_pool(name="keep", bufs=1))
+        work = ctx.enter_context(tc.tile_pool(name="work", bufs=2))
+        psum = ctx.enter_context(tc.psum_pool(name="psum", bufs=1))
+        turn = ctx.enter_context(tc.psum_pool(name="turn", bufs=3))
+
+        offsets = keep.tile([P, J // 16], U16, name="offsets")
+        nc.sync.dma_start(offsets[:], offs)
+        rb_cols = keep.tile([P, 4], F32, name="rb_cols")
+        nc.sync.dma_start(rb_cols[:], rb.rearrange("o (p t) -> (o p) t", t=4))
+
+        def load(src, b, width, name):
+            tile = keep.tile([P, width], F32, name=f"{name}{b}")
+            nc.sync.dma_start(tile[:], src[b * P : (b + 1) * P, :])
+            return tile
+
+        g_sb, sv_sb, x_sb, mom_sb = {}, {}, {}, {}
+        for name in "g0 s0 x0 g1 s1 x1 g2 s2 x2 g3 s3 x3 m0 m1 m2 m3".split():
+            b = int(name[1])
+            if name[0] == "g":
+                g_sb[b] = load(g, b, T, "g")
+            elif name[0] == "s":
+                sv_sb[b] = load(sv, b, T, "sv")
+            elif name[0] == "x":
+                x_sb[b] = load(xt, b, T, "x")
+            else:
+                mom_sb[b] = load(mom, b, N, "mom")
+
+        ident = keep.tile([P, P], F32, name="ident")
+        make_identity(nc, ident[:])
+
+        rb_ps = psum.tile([P, 4, P], F32, name="rb_ps")
+        for t in range(4):
+            nc.tensor.transpose(rb_ps[:, t, :], rb_cols[:, t : t + 1].to_broadcast([P, P]), ident[:])
+        rb_all = keep.tile([P, J], F32, name="rb_all")
+        nc.vector.tensor_copy(rb_all[:].rearrange("q (p t) -> q p t", t=4), rb_ps[:].rearrange("q t p -> q p t"))
+
+        g_codes = keep.tile([P, N], U32, name="g_codes", align_bytes=64)
+        g_scales = keep.tile([P, N], U8, name="g_scales", align_bytes=64)
+
+        def turn_block(values, name):
+            words = values[:].bitcast(F32)
+            turned = turn.tile([P, 2, P], F32, name="turned")
+            for u in range(2):
+                nc.tensor.transpose(turned[:, u, :], words[:, u : J // 2 : 2], ident[:])
+            grouped = keep.tile([P, 4 * P], BF16, name=name, align_bytes=64)
+            nc.scalar.copy(
+                grouped[:].bitcast(F32).rearrange("p (c u) -> p c u", u=2),
+                turned[:].rearrange("p u c -> p c u"),
+            )
+            return grouped
+
+        def gather_g(b):
+            weighted = work.tile([P, J], F32, name="weighted")
+            nc.vector.tensor_tensor(weighted[:], g_sb[b][:].indirect(offsets[:]), rb_all[:], MULT)
+            product = work.tile([P, J], F32, name="product")
+            nc.vector.tensor_tensor(product[:], sv_sb[b][:].indirect(offsets[:]), weighted[:], MULT)
+            rounded = work.tile([P, J], BF16, name="rounded")
+            nc.scalar.activation(rounded[:], product[:], COPY)
+            return turn_block(rounded, f"g_grouped{b}")
+
+        def quantize_g(b, grouped):
+            cols = slice(b * P, (b + 1) * P)
+            nc.vector.quantize_mx(out=g_codes[:, cols].bitcast(E5M2), scales=g_scales[:, cols], in_=grouped[:])
+
+        def gather_x(b):
+            picked = work.tile([P, J], BF16, name="picked")
+            if b < SCALAR_BLOCKS:
+                x_bf = work.tile([P, T], BF16, name="x_bf")
+                nc.scalar.activation(x_bf[:], x_sb[b][:], COPY)
+                nc.scalar.activation(picked[:], x_bf[:].indirect(offsets[:]), COPY)
+            else:
+                nc.vector.tensor_copy(picked[:], x_sb[b][:].indirect(offsets[:]))
+            return turn_block(picked, f"x_grouped{b}")
+
+        def quantize_x(b, grouped):
+            codes = keep.tile([P, P], U32, name=f"x_codes{b}", align_bytes=64)
+            scales = keep.tile([P, P], U8, name=f"x_scales{b}", align_bytes=64)
+            nc.vector.quantize_mx(out=codes[:].bitcast(E4M3), scales=scales[:], in_=grouped[:])
+            return codes, scales
+
+        def finish(b, codes, scales):
+            acc = psum.tile([P, N], F32, name=f"acc{b}")
+            nc.tensor.matmul_mx(
+                out=acc[:],
+                lhsT=codes[:].bitcast(E4M3),
+                lhsT_scale=scales[:],
+                rhs=g_codes[:].bitcast(E5M2),
+                rhs_scale=g_scales[:],
+                start=True,
+                stop=True,
+            )
+            half_mom = keep.tile([P, N], F32, name=f"half_mom{b}")
+            nc.scalar.mul(half_mom[:], mom_sb[b][:], 0.5)
+            result = keep.tile([P, N], F32, name=f"result{b}")
+            nc.vector.scalar_tensor_tensor(result[:], acc[:], 0.04, half_mom[:], MULT, ADD)
+            nc.sync.dma_start(out[b * P : (b + 1) * P, :], result[:])
+
+        g_grouped, x_grouped, x_mx = {}, {}, {}
+        for step in "G0 X0 G1 g0 X1 x0 G2 g1 X2 x1 G3 g2 X3 x2 g3 F0 x3 F1 F2 F3".split():
+            b = int(step[1])
+            if step[0] == "G":
+                g_grouped[b] = gather_g(b)
+            elif step[0] == "g":
+                quantize_g(b, g_grouped[b])
+            elif step[0] == "X":
+                x_grouped[b] = gather_x(b)
+            elif step[0] == "x":
+                x_mx[b] = quantize_x(b, x_grouped[b])
+            else:
+                finish(b, *x_mx[b])

@@ -19,119 +19,144 @@ COPY = mybir.ActivationFunctionType.Copy
 
 P = 128
 BLOCKS = 4
-SCALAR_BLOCKS = 3
+SCALAR_X = (1, 2)
+WORD_G = (0, 1, 2, 3)
 
 
 def tile_moe_expert_wgrad_through_saved_kernel(tc, xt, g, sv, rb, mom, offs, out):
     nc = tc.nc
     with ExitStack() as ctx:
         keep = ctx.enter_context(tc.tile_pool(name="keep", bufs=1))
-        work = ctx.enter_context(tc.tile_pool(name="work", bufs=2))
-        psum = ctx.enter_context(tc.psum_pool(name="psum", bufs=1))
-        turn = ctx.enter_context(tc.psum_pool(name="turn", bufs=3))
+        work = ctx.enter_context(tc.tile_pool(name="work", bufs=4))
+        psum = ctx.enter_context(tc.psum_pool(name="psum", bufs=8))
 
-        offsets = keep.tile([P, J // 16], U16, name="offsets")
-        nc.sync.dma_start(offsets[:], offs)
         rb_cols = keep.tile([P, 4], F32, name="rb_cols")
         nc.sync.dma_start(rb_cols[:], rb.rearrange("o (p t) -> (o p) t", t=4))
+        offsets = keep.tile([P, J // 16], U16, name="offsets")
+        nc.sync.dma_start(offsets[:], offs)
 
-        def load(src, b, width, name):
-            tile = keep.tile([P, width], F32, name=f"{name}{b}")
-            nc.sync.dma_start(tile[:], src[b * P : (b + 1) * P, :])
-            return tile
-
-        g_sb, sv_sb, x_sb, mom_sb = {}, {}, {}, {}
-        for name in "g0 s0 x0 g1 s1 x1 g2 s2 x2 g3 s3 x3 m0 m1 m2 m3".split():
+        sb = {}
+        for name in "x0 g0 g1 x1 s0 s1 g2 x2 g3 s2 s3 x3 m0 m1 m2 m3".split():
             b = int(name[1])
-            if name[0] == "g":
-                g_sb[b] = load(g, b, T, "g")
-            elif name[0] == "s":
-                sv_sb[b] = load(sv, b, T, "sv")
-            elif name[0] == "x":
-                x_sb[b] = load(xt, b, T, "x")
-            else:
-                mom_sb[b] = load(mom, b, N, "mom")
+            src = {"g": g, "s": sv, "x": xt, "m": mom}[name[0]]
+            sb[name] = keep.tile([P, src.shape[1]], F32, name=name, tag=name, align_bytes=64)
+            nc.sync.dma_start(sb[name][:], src[b * P : (b + 1) * P, :])
 
         ident = keep.tile([P, P], F32, name="ident")
         make_identity(nc, ident[:])
 
-        rb_ps = psum.tile([P, 4, P], F32, name="rb_ps")
+        rb_ps = psum.tile([P, 4, P], F32, name="rb_ps", tag="bank")
         for t in range(4):
             nc.tensor.transpose(rb_ps[:, t, :], rb_cols[:, t : t + 1].to_broadcast([P, P]), ident[:])
         rb_all = keep.tile([P, J], F32, name="rb_all")
         nc.vector.tensor_copy(rb_all[:].rearrange("q (p t) -> q p t", t=4), rb_ps[:].rearrange("q t p -> q p t"))
 
-        g_codes = keep.tile([P, N], U32, name="g_codes", align_bytes=64)
+        g_codes = keep.tile([P, N], U32, name="g_codes", tag="x3", align_bytes=64)
         g_scales = keep.tile([P, N], U8, name="g_scales", align_bytes=64)
+        x_codes = keep.tile([P, K], U32, name="x_codes", tag="s3", align_bytes=64)
+        x_scales = keep.tile([P, K], U8, name="x_scales", align_bytes=64)
+        weighted = [keep.tile([P, J], F32, name=f"weighted{i}") for i in range(2)]
+        late = {}
+        x_bf = keep.tile([P, T], BF16, name="x_bf", tag="x_bf")
 
-        def turn_block(values, name):
-            words = values[:].bitcast(F32)
-            turned = turn.tile([P, 2, P], F32, name="turned")
+        def grouped_blocks(side, first, last):
+            key = f"{side}_grouped{first // 2}"
+            if key not in late:
+                tag = {"g_grouped1": "product3", "x_grouped1": "product2"}.get(key, key)
+                late[key] = keep.tile([P, 8 * P], BF16, name=key, tag=tag, align_bytes=64)
+            return late[key][:, (first % 2) * 4 * P : (last % 2 + 1) * 4 * P]
+
+        def turn_words(halves, grouped, last):
+            if not last:
+                turned = psum.tile([P, 2, P], F32, name="turned", tag="bank")
+            else:
+                if "turned" not in late:
+                    late["turned"] = psum.tile([P, 2, P], F32, name="turned", tag="bank")
+                turned = late["turned"]
             for u in range(2):
-                nc.tensor.transpose(turned[:, u, :], words[:, u : J // 2 : 2], ident[:])
-            grouped = keep.tile([P, 4 * P], BF16, name=name, align_bytes=64)
+                nc.tensor.transpose(turned[:, u, :], halves[u], ident[:])
+            late[grouped] = turned
+
+        def empty_bank(side, b):
+            turned = late[(side, b)]
             nc.scalar.copy(
-                grouped[:].bitcast(F32).rearrange("p (c u) -> p c u", u=2),
+                grouped_blocks(side, b, b).bitcast(F32).rearrange("p (c u) -> p c u", u=2),
                 turned[:].rearrange("p u c -> p c u"),
             )
-            return grouped
+
+        def gather_w(b):
+            nc.vector.tensor_tensor(weighted[b % 2][:], sb[f"g{b}"][:].indirect(offsets[:]), rb_all[:], MULT)
 
         def gather_g(b):
-            weighted = work.tile([P, J], F32, name="weighted")
-            nc.vector.tensor_tensor(weighted[:], g_sb[b][:].indirect(offsets[:]), rb_all[:], MULT)
-            product = work.tile([P, J], F32, name="product")
-            nc.vector.tensor_tensor(product[:], sv_sb[b][:].indirect(offsets[:]), weighted[:], MULT)
-            rounded = work.tile([P, J], BF16, name="rounded")
-            nc.scalar.activation(rounded[:], product[:], COPY)
-            return turn_block(rounded, f"g_grouped{b}")
-
-        def quantize_g(b, grouped):
-            cols = slice(b * P, (b + 1) * P)
-            nc.vector.quantize_mx(out=g_codes[:, cols].bitcast(E5M2), scales=g_scales[:, cols], in_=grouped[:])
+            product = keep.tile([P, J], F32, name=f"product{b}", tag=f"product{b}", align_bytes=64)
+            nc.vector.tensor_tensor(product[:], sb[f"s{b}"][:].indirect(offsets[:]), weighted[b % 2][:], MULT)
+            if b in WORD_G:
+                if b < 2:
+                    rounded = work.tile([P, J], BF16, name="rounded")
+                else:
+                    if "rounded" not in late:
+                        late["rounded"] = keep.tile([P, 2 * J], BF16, name="rounded_late", tag="x_bf")
+                    rounded = late["rounded"][:, (b % 2) * J : (b % 2 + 1) * J]
+                nc.scalar.activation(
+                    rounded[:].rearrange("q (u p e) -> q u p e", u=2, e=2),
+                    product[:].rearrange("q (p u e) -> q u p e", u=2, e=2),
+                    COPY,
+                )
+                words = rounded[:].bitcast(F32)
+                turn_words([words[:, u * P : (u + 1) * P] for u in range(2)], ("g", b), b == 3)
 
         def gather_x(b):
-            picked = work.tile([P, J], BF16, name="picked")
-            if b < SCALAR_BLOCKS:
-                x_bf = work.tile([P, T], BF16, name="x_bf")
-                nc.scalar.activation(x_bf[:], x_sb[b][:], COPY)
-                nc.scalar.activation(picked[:], x_bf[:].indirect(offsets[:]), COPY)
+            if b in SCALAR_X:
+                picked = work.tile([P, J], BF16, name="picked")[:]
+                nc.scalar.activation(x_bf[:], sb[f"x{b}"][:], COPY)
+                nc.scalar.activation(picked, x_bf[:].indirect(offsets[:]), COPY)
             else:
-                nc.vector.tensor_copy(picked[:], x_sb[b][:].indirect(offsets[:]))
-            return turn_block(picked, f"x_grouped{b}")
+                picked = weighted[0][:, : J // 2].bitcast(BF16) if b else work.tile([P, J], BF16, name="picked")[:]
+                nc.vector.tensor_copy(picked, sb[f"x{b}"][:].indirect(offsets[:]))
+            words = picked.bitcast(F32)
+            turn_words([words[:, u : J // 2 : 2] for u in range(2)], ("x", b), b == 3)
 
-        def quantize_x(b, grouped):
-            codes = keep.tile([P, P], U32, name=f"x_codes{b}", align_bytes=64)
-            scales = keep.tile([P, P], U8, name=f"x_scales{b}", align_bytes=64)
-            nc.vector.quantize_mx(out=codes[:].bitcast(E4M3), scales=scales[:], in_=grouped[:])
-            return codes, scales
+        def quantize(grouped, codes, scales, fmt, first, last):
+            cols = slice(first * P, (last + 1) * P)
+            nc.vector.quantize_mx(
+                out=codes[:, cols].bitcast(fmt),
+                scales=scales[:, cols],
+                in_=grouped_blocks(grouped, first, last),
+            )
 
-        def finish(b, codes, scales):
-            acc = psum.tile([P, N], F32, name=f"acc{b}")
+        def finish(b):
+            cols = slice(b * P, (b + 1) * P)
+            acc = psum.tile([P, N], F32, name="acc", tag="bank")
             nc.tensor.matmul_mx(
                 out=acc[:],
-                lhsT=codes[:].bitcast(E4M3),
-                lhsT_scale=scales[:],
+                lhsT=x_codes[:, cols].bitcast(E4M3),
+                lhsT_scale=x_scales[:, cols],
                 rhs=g_codes[:].bitcast(E5M2),
                 rhs_scale=g_scales[:],
                 start=True,
                 stop=True,
             )
             half_mom = keep.tile([P, N], F32, name=f"half_mom{b}")
-            nc.scalar.mul(half_mom[:], mom_sb[b][:], 0.5)
+            nc.gpsimd.tensor_scalar(half_mom[:], sb[f"m{b}"][:], 0.5, 0.0, MULT, ADD)
             result = keep.tile([P, N], F32, name=f"result{b}")
             nc.vector.scalar_tensor_tensor(result[:], acc[:], 0.04, half_mom[:], MULT, ADD)
             nc.sync.dma_start(out[b * P : (b + 1) * P, :], result[:])
 
-        g_grouped, x_grouped, x_mx = {}, {}, {}
-        for step in "G0 X0 G1 g0 X1 x0 G2 g1 X2 x1 G3 g2 X3 x2 g3 F0 x3 F1 F2 F3".split():
+        for step in "X0 D0 W0 W1 X1 D1 G0 E0 G1 E1 W2 X2 W3 G2 D2 G3 E2 E3 X3 D3 g01 x01 g2 g3 F0 x23 F1 F2 F3".split():
             b = int(step[1])
-            if step[0] == "G":
-                g_grouped[b] = gather_g(b)
+            if step[0] == "E":
+                empty_bank("g", b)
+            elif step[0] == "D":
+                empty_bank("x", b)
+            elif step[0] == "W":
+                gather_w(b)
+            elif step[0] == "G":
+                gather_g(b)
             elif step[0] == "g":
-                quantize_g(b, g_grouped[b])
+                quantize("g", g_codes, g_scales, E5M2, b, int(step[-1]))
             elif step[0] == "X":
-                x_grouped[b] = gather_x(b)
+                gather_x(b)
             elif step[0] == "x":
-                x_mx[b] = quantize_x(b, x_grouped[b])
+                quantize("x", x_codes, x_scales, E4M3, b, int(step[-1]))
             else:
-                finish(b, *x_mx[b])
+                finish(b)

@@ -19,7 +19,7 @@ COPY = mybir.ActivationFunctionType.Copy
 
 P = 128
 BLOCKS = 4
-SCALAR_X = (1, 2)
+SCALAR_X = (1,)
 WORD_G = (0, 1, 2, 3)
 
 
@@ -36,7 +36,7 @@ def tile_moe_expert_wgrad_through_saved_kernel(tc, xt, g, sv, rb, mom, offs, out
         nc.sync.dma_start(offsets[:], offs)
 
         sb = {}
-        for name in "x0 g0 g1 x1 s0 s1 g2 x2 g3 s2 s3 x3 m0 m1 m2 m3".split():
+        for name in "x0 g0 g1 s0 s1 x1 g2 g3 s2 s3 x2 x3 m0 m1 m2 m3".split():
             b = int(name[1])
             src = {"g": g, "s": sv, "x": xt, "m": mom}[name[0]]
             sb[name] = keep.tile([P, src.shape[1]], F32, name=name, tag=name, align_bytes=64)
@@ -51,7 +51,7 @@ def tile_moe_expert_wgrad_through_saved_kernel(tc, xt, g, sv, rb, mom, offs, out
         rb_all = keep.tile([P, J], F32, name="rb_all")
         nc.vector.tensor_copy(rb_all[:].rearrange("q (p t) -> q p t", t=4), rb_ps[:].rearrange("q t p -> q p t"))
 
-        g_codes = keep.tile([P, N], U32, name="g_codes", tag="x3", align_bytes=64)
+        g_codes = keep.tile([P, N], U32, name="g_codes", tag="x2", align_bytes=64)
         g_scales = keep.tile([P, N], U8, name="g_scales", align_bytes=64)
         x_codes = keep.tile([P, K], U32, name="x_codes", tag="s3", align_bytes=64)
         x_scales = keep.tile([P, K], U8, name="x_scales", align_bytes=64)
@@ -62,7 +62,7 @@ def tile_moe_expert_wgrad_through_saved_kernel(tc, xt, g, sv, rb, mom, offs, out
         def grouped_blocks(side, first, last):
             key = f"{side}_grouped{first // 2}"
             if key not in late:
-                tag = {"g_grouped1": "product3", "x_grouped1": "product2"}.get(key, key)
+                tag = {"g_grouped1": "product3"}.get(key, key)
                 late[key] = keep.tile([P, 8 * P], BF16, name=key, tag=tag, align_bytes=64)
             return late[key][:, (first % 2) * 4 * P : (last % 2 + 1) * 4 * P]
 
@@ -91,12 +91,7 @@ def tile_moe_expert_wgrad_through_saved_kernel(tc, xt, g, sv, rb, mom, offs, out
             product = keep.tile([P, J], F32, name=f"product{b}", tag=f"product{b}", align_bytes=64)
             nc.vector.tensor_tensor(product[:], sb[f"s{b}"][:].indirect(offsets[:]), weighted[b % 2][:], MULT)
             if b in WORD_G:
-                if b < 2:
-                    rounded = work.tile([P, J], BF16, name="rounded")
-                else:
-                    if "rounded" not in late:
-                        late["rounded"] = keep.tile([P, 2 * J], BF16, name="rounded_late", tag="x_bf")
-                    rounded = late["rounded"][:, (b % 2) * J : (b % 2 + 1) * J]
+                rounded = keep.tile([P, J], BF16, name=f"rounded{b}", tag=f"rounded{b}")
                 nc.scalar.activation(
                     rounded[:].rearrange("q (u p e) -> q u p e", u=2, e=2),
                     product[:].rearrange("q (p u e) -> q u p e", u=2, e=2),
@@ -111,10 +106,10 @@ def tile_moe_expert_wgrad_through_saved_kernel(tc, xt, g, sv, rb, mom, offs, out
                 nc.scalar.activation(x_bf[:], sb[f"x{b}"][:], COPY)
                 nc.scalar.activation(picked, x_bf[:].indirect(offsets[:]), COPY)
             else:
-                picked = weighted[0][:, : J // 2].bitcast(BF16) if b else work.tile([P, J], BF16, name="picked")[:]
+                picked = keep.tile([P, J], BF16, name=f"picked{b}", tag=f"picked{b}")[:]
                 nc.vector.tensor_copy(picked, sb[f"x{b}"][:].indirect(offsets[:]))
             words = picked.bitcast(F32)
-            turn_words([words[:, u : J // 2 : 2] for u in range(2)], ("x", b), b == 3)
+            turn_words([words[:, u : J // 2 : 2] for u in range(2)], ("x", b), b >= 2)
 
         def quantize(grouped, codes, scales, fmt, first, last):
             cols = slice(first * P, (last + 1) * P)
@@ -136,13 +131,20 @@ def tile_moe_expert_wgrad_through_saved_kernel(tc, xt, g, sv, rb, mom, offs, out
                 start=True,
                 stop=True,
             )
-            half_mom = keep.tile([P, N], F32, name=f"half_mom{b}")
-            nc.gpsimd.tensor_scalar(half_mom[:], sb[f"m{b}"][:], 0.5, 0.0, MULT, ADD)
-            result = keep.tile([P, N], F32, name=f"result{b}")
-            nc.vector.scalar_tensor_tensor(result[:], acc[:], 0.04, half_mom[:], MULT, ADD)
-            nc.sync.dma_start(out[b * P : (b + 1) * P, :], result[:])
+            key = f"half_mom{b // 2}"
+            if key not in late:
+                late[key] = keep.tile([P, 2 * N], F32, name=key, tag=("rounded3", "picked3")[b // 2])
+            half_mom = late[key][:, (b % 2) * N : (b % 2 + 1) * N]
+            nc.scalar.mul(half_mom, sb[f"m{b}"][:], 0.5)
+            parts = 2 if b == BLOCKS - 1 else 1
+            for h in range(parts):
+                part = slice(h * N // parts, (h + 1) * N // parts)
+                result = keep.tile([P, N // parts], F32, name=f"result{b}_{h}")
+                nc.vector.scalar_tensor_tensor(result[:], acc[:, part], 0.04, half_mom[:, part], MULT, ADD)
+                queue = nc.scalar if h else nc.sync
+                queue.dma_start(out[b * P : (b + 1) * P, part], result[:])
 
-        for step in "X0 D0 W0 W1 X1 D1 G0 E0 G1 E1 W2 X2 W3 G2 D2 G3 E2 E3 X3 D3 g01 x01 g2 g3 F0 x23 F1 F2 F3".split():
+        for step in "X0 D0 W0 W1 G0 E0 G1 E1 X1 D1 W2 W3 G2 G3 E2 E3 X2 D2 x01 g01 g23 X3 D3 x2 F0 F1 x3 F2 F3".split():
             b = int(step[1])
             if step[0] == "E":
                 empty_bank("g", b)

from contextlib import ExitStack

import concourse.mybir as mybir
from concourse.masks import make_identity

K, N, T, J = 512, 512, 1024, 512
FLOPS = 2 * K * N * J

F32 = mybir.dt.float32
BF16 = mybir.dt.bfloat16
U32 = mybir.dt.uint32
U16 = mybir.dt.uint16
U8 = mybir.dt.uint8
E4M3 = mybir.dt.float8_e4m3fn_x4
E5M2 = mybir.dt.float8_e5m2_x4
MULT = mybir.AluOpType.mult
ADD = mybir.AluOpType.add
COPY = mybir.ActivationFunctionType.Copy

P = 128
BLOCKS = 4
SCALAR_X = (1,)
WORD_G = (0, 1, 2, 3)


def tile_moe_expert_wgrad_through_saved_kernel(tc, xt, g, sv, rb, mom, offs, out):
    nc = tc.nc
    with ExitStack() as ctx:
        keep = ctx.enter_context(tc.tile_pool(name="keep", bufs=1))
        work = ctx.enter_context(tc.tile_pool(name="work", bufs=4))
        psum = ctx.enter_context(tc.psum_pool(name="psum", bufs=8))

        rb_cols = keep.tile([P, 4], F32, name="rb_cols")
        nc.sync.dma_start(rb_cols[:], rb.rearrange("o (p t) -> (o p) t", t=4))
        offsets = keep.tile([P, J // 16], U16, name="offsets")
        nc.sync.dma_start(offsets[:], offs)

        sb = {}
        for name in "x0 g0 g1 s0 s1 x1 g2 g3 s2 s3 x2 x3 m0 m1 m2 m3".split():
            b = int(name[1])
            src = {"g": g, "s": sv, "x": xt, "m": mom}[name[0]]
            sb[name] = keep.tile([P, src.shape[1]], F32, name=name, tag=name, align_bytes=64)
            nc.sync.dma_start(sb[name][:], src[b * P : (b + 1) * P, :])

        ident = keep.tile([P, P], F32, name="ident")
        make_identity(nc, ident[:])

        rb_ps = psum.tile([P, 4, P], F32, name="rb_ps", tag="bank")
        for t in range(4):
            nc.tensor.transpose(rb_ps[:, t, :], rb_cols[:, t : t + 1].to_broadcast([P, P]), ident[:])
        rb_all = keep.tile([P, J], F32, name="rb_all")
        nc.vector.tensor_copy(rb_all[:].rearrange("q (p t) -> q p t", t=4), rb_ps[:].rearrange("q t p -> q p t"))

        g_codes = keep.tile([P, N], U32, name="g_codes", tag="x2", align_bytes=64)
        g_scales = keep.tile([P, N], U8, name="g_scales", align_bytes=64)
        x_codes = keep.tile([P, K], U32, name="x_codes", tag="s3", align_bytes=64)
        x_scales = keep.tile([P, K], U8, name="x_scales", align_bytes=64)
        weighted = [keep.tile([P, J], F32, name=f"weighted{i}") for i in range(2)]
        late = {}
        x_bf = keep.tile([P, T], BF16, name="x_bf", tag="x_bf")

        def grouped_blocks(side, first, last):
            key = f"{side}_grouped{first // 2}"
            if key not in late:
                tag = {"g_grouped1": "product3"}.get(key, key)
                late[key] = keep.tile([P, 8 * P], BF16, name=key, tag=tag, align_bytes=64)
            return late[key][:, (first % 2) * 4 * P : (last % 2 + 1) * 4 * P]

        def turn_words(halves, grouped, last):
            if not last:
                turned = psum.tile([P, 2, P], F32, name="turned", tag="bank")
            else:
                if "turned" not in late:
                    late["turned"] = psum.tile([P, 2, P], F32, name="turned", tag="bank")
                turned = late["turned"]
            for u in range(2):
                nc.tensor.transpose(turned[:, u, :], halves[u], ident[:])
            late[grouped] = turned

        def empty_bank(side, b):
            turned = late[(side, b)]
            nc.scalar.copy(
                grouped_blocks(side, b, b).bitcast(F32).rearrange("p (c u) -> p c u", u=2),
                turned[:].rearrange("p u c -> p c u"),
            )

        def gather_w(b):
            nc.vector.tensor_tensor(weighted[b % 2][:], sb[f"g{b}"][:].indirect(offsets[:]), rb_all[:], MULT)

        def gather_g(b):
            product = keep.tile([P, J], F32, name=f"product{b}", tag=f"product{b}", align_bytes=64)
            nc.vector.tensor_tensor(product[:], sb[f"s{b}"][:].indirect(offsets[:]), weighted[b % 2][:], MULT)
            if b in WORD_G:
                rounded = keep.tile([P, J], BF16, name=f"rounded{b}", tag=f"rounded{b}")
                nc.scalar.activation(
                    rounded[:].rearrange("q (u p e) -> q u p e", u=2, e=2),
                    product[:].rearrange("q (p u e) -> q u p e", u=2, e=2),
                    COPY,
                )
                words = rounded[:].bitcast(F32)
                turn_words([words[:, u * P : (u + 1) * P] for u in range(2)], ("g", b), b == 3)

        def gather_x(b):
            if b in SCALAR_X:
                picked = work.tile([P, J], BF16, name="picked")[:]
                nc.scalar.activation(x_bf[:], sb[f"x{b}"][:], COPY)
                nc.scalar.activation(picked, x_bf[:].indirect(offsets[:]), COPY)
            else:
                picked = keep.tile([P, J], BF16, name=f"picked{b}", tag=f"picked{b}")[:]
                nc.vector.tensor_copy(picked, sb[f"x{b}"][:].indirect(offsets[:]))
            words = picked.bitcast(F32)
            turn_words([words[:, u : J // 2 : 2] for u in range(2)], ("x", b), b >= 2)

        def quantize(grouped, codes, scales, fmt, first, last):
            cols = slice(first * P, (last + 1) * P)
            nc.vector.quantize_mx(
                out=codes[:, cols].bitcast(fmt),
                scales=scales[:, cols],
                in_=grouped_blocks(grouped, first, last),
            )

        def finish(b):
            cols = slice(b * P, (b + 1) * P)
            acc = psum.tile([P, N], F32, name="acc", tag="bank")
            nc.tensor.matmul_mx(
                out=acc[:],
                lhsT=x_codes[:, cols].bitcast(E4M3),
                lhsT_scale=x_scales[:, cols],
                rhs=g_codes[:].bitcast(E5M2),
                rhs_scale=g_scales[:],
                start=True,
                stop=True,
            )
            key = f"half_mom{b // 2}"
            if key not in late:
                late[key] = keep.tile([P, 2 * N], F32, name=key, tag=("rounded3", "picked3")[b // 2])
            half_mom = late[key][:, (b % 2) * N : (b % 2 + 1) * N]
            nc.scalar.mul(half_mom, sb[f"m{b}"][:], 0.5)
            parts = 2 if b == BLOCKS - 1 else 1
            for h in range(parts):
                part = slice(h * N // parts, (h + 1) * N // parts)
                result = keep.tile([P, N // parts], F32, name=f"result{b}_{h}")
                nc.vector.scalar_tensor_tensor(result[:], acc[:, part], 0.04, half_mom[:, part], MULT, ADD)
                queue = nc.scalar if h else nc.sync
                queue.dma_start(out[b * P : (b + 1) * P, part], result[:])

        for step in "X0 D0 W0 W1 G0 E0 G1 E1 X1 D1 W2 W3 G2 G3 E2 E3 X2 D2 x01 g01 g23 X3 D3 x2 F0 F1 x3 F2 F3".split():
            b = int(step[1])
            if step[0] == "E":
                empty_bank("g", b)
            elif step[0] == "D":
                empty_bank("x", b)
            elif step[0] == "W":
                gather_w(b)
            elif step[0] == "G":
                gather_g(b)
            elif step[0] == "g":
                quantize("g", g_codes, g_scales, E5M2, b, int(step[-1]))
            elif step[0] == "X":
                gather_x(b)
            elif step[0] == "x":
                quantize("x", x_codes, x_scales, E4M3, b, int(step[-1]))
            else:
                finish(b)
